import numpy as np
import ml_dtypes


def mxq(x, axis, fmt="e4m3"):
    dtype, down = {"e4m3": (ml_dtypes.float8_e4m3fn, 7), "e5m2": (ml_dtypes.float8_e5m2, 14)}[fmt]
    v = np.moveaxis(np.asarray(x, np.float32).astype(ml_dtypes.bfloat16).astype(np.float64), axis, -1)
    blocks = v.reshape(v.shape[:-1] + (-1, 32))
    amax = np.abs(blocks).max(-1, keepdims=True)
    byte = np.maximum(np.where(amax > 0, np.frexp(amax)[1] - 1 + 127, 0) - down, 1)
    scale = np.exp2(byte - 127.0)
    codes = (blocks / scale).astype(np.float32).astype(dtype).astype(np.float64)
    return np.moveaxis((codes * scale).reshape(v.shape), -1, axis)


WIDE = False


def mx_kscale(k):
    if not WIDE:
        return np.ones(k)
    levels = np.array([10, -10, 5, -5, 0])
    if k % 512:
        return np.exp2(np.random.permutation(np.resize(levels, k // 32))).repeat(32)
    a = np.empty((k // 512, 16))
    for p in range(k // 512):
        a[p, :8] = np.random.permutation(np.resize(levels, 8))
        for g in range(8):
            far = levels[np.abs(levels - a[p, g]) >= 10]
            a[p, g + 8] = far[np.random.randint(len(far))]
    return np.exp2(a.ravel()).repeat(32)


def f64(x):
    return np.asarray(x).astype(np.float64)


def striped(idx):
    return np.tile(np.asarray(idx).reshape(-1, 16).T, (8, 1)).astype(np.uint16)


def unstriped(offs):
    return offs[:16].T.reshape(-1).astype(np.int64)


E2M1 = np.array([0.0, 0.5, 1.0, 1.5, 2.0, 3.0, 4.0, 6.0, -0.0, -0.5, -1.0, -1.5, -2.0, -3.0, -4.0, -6.0])


def pack_weight(w, fmt):
    k, n = w.shape
    w = f64(np.asarray(w, np.float32).astype(ml_dtypes.bfloat16)).reshape(k // 32, 32, n)
    amax = np.abs(w).max(1)
    if fmt == "e4m3":
        byte = np.frexp(amax)[1] - 1 + 127 - 7
    else:
        mant, ex = np.frexp(amax / 6.0)
        byte = np.where(mant > 0.5, ex, ex - 1) + 127
    byte = np.clip(np.where(amax > 0, byte, 1), 1, 254)
    scaled = (w * np.exp2(127.0 - byte)[:, None, :]).reshape(k, n).astype(np.float32)
    by_word = np.ascontiguousarray(scaled.reshape(k // 512, 128, 4, n).transpose(0, 1, 3, 2))
    if fmt == "e4m3":
        words = by_word.astype(ml_dtypes.float8_e4m3fn).view(np.uint8)
    else:
        c = by_word.astype(ml_dtypes.float4_e2m1fn).view(np.uint8) & 0xF
        words = (c[..., 0::2] | (c[..., 1::2] << 4)).reshape(k // 512, 128, 2 * n)
    return np.ascontiguousarray(words), np.ascontiguousarray(byte.astype(np.uint8).reshape(k // 512, 16, n))


def unpack_weight(words, scales, fmt):
    g, _, n = scales.shape
    words = np.ascontiguousarray(words).reshape(g, 128, n, -1)
    if fmt == "e4m3":
        vals = words.view(ml_dtypes.float8_e4m3fn).astype(np.float64)
    else:
        nib = np.empty((g, 128, n, 4), np.uint8)
        nib[..., 0::2] = words & 0xF
        nib[..., 1::2] = words >> 4
        vals = E2M1[nib]
    vals = vals * np.repeat(np.exp2(scales.astype(np.float64) - 127.0), 8, axis=1)[..., None]
    return vals.transpose(0, 1, 3, 2).reshape(g * 512, n)


def sigmoid(v):
    return 1.0 / (1.0 + np.exp(-v))


D, E, T, I, Q = 512, 512, 2048, 512, 128


def setup_inputs():
    n = np.random.standard_normal
    idx = np.random.permutation(T)[:I]
    fd = mx_kscale(D)
    fe = mx_kscale(E)
    keysp = pack_weight(n((D, T)) / fd[:, None], "e2m1")
    valsp = pack_weight(n((E, T)) / fe[:, None], "e2m1")
    return {
        "query": (n((D, Q)) * 0.8 / np.sqrt(D) * fd[:, None]).astype(np.float32),
        "keys_words": keysp[0],
        "keys_scales": keysp[1],
        "share": (np.random.uniform(0.2, 0.8, (Q, 1))).astype(np.float32),
        "gout": (n((E, Q)) * 1 / np.sqrt(E) * fe[:, None]).astype(np.float32),
        "vals_words": valsp[0],
        "vals_scales": valsp[1],
        "old": (0.5 * n((Q, T))).astype(np.float32),
        "offs": striped(idx),
    }


def reference(query, keys_words, keys_scales, share, gout, vals_words, vals_scales, old, offs):
    idx = unstriped(offs)
    keysu = unpack_weight(keys_words, keys_scales, "e2m1")
    valsu = unpack_weight(vals_words, vals_scales, "e2m1")
    queryq = mxq(f64(query), 0, "e4m3")
    keysidxg = keysu[:, idx]
    a = queryq.T @ keysidxg
    e0 = np.exp(a)
    s0 = sigmoid(a)
    p = e0 * f64(share) + s0 * (1.0 - f64(share)) * 3.0
    z = np.sum(p, axis=1, keepdims=True)
    goutq = mxq(f64(gout), 0, "e4m3")
    valsidxg = valsu[:, idx]
    c0 = goutq.T @ valsidxg
    dz = np.sum(c0 * p / np.square(z) * (-1.0), axis=1, keepdims=True)
    dp = c0 / z + dz
    ds0 = dp * 3.0 * (1.0 - f64(share))
    de0 = dp * f64(share)
    da = ds0 * s0 * (1.0 - s0) + de0 * e0
    gs = da * 512.0
    gf = np.zeros((Q, T))
    gf[:, idx] = gs
    y = f64(old) + gf
    return y

@@ -1,0 +1,146 @@
+from contextlib import ExitStack
+
+import concourse.mybir as mybir
+
+D, E, T, I, Q = 512, 512, 2048, 512, 128
+FLOPS = 2 * Q * I * (D + E)
+
+F32 = mybir.dt.float32
+BF16 = mybir.dt.bfloat16
+I32 = mybir.dt.int32
+U32 = mybir.dt.uint32
+U16 = mybir.dt.uint16
+U8 = mybir.dt.uint8
+FP8X4 = mybir.dt.float8_e4m3fn_x4
+FP4X4 = mybir.dt.float4_e2m1fn_x4
+ALU = mybir.AluOpType
+ACT = mybir.ActivationFunctionType
+
+P = 128
+PACK = 4
+HALF = I // 2
+STORE_WIDTHS = (256, 512, 512, 512, 256)
+
+
+def tile_attend_bmixedparts_s_kernel(tc, query, keys_words, keys_scales, share, gout, vals_words, vals_scales, old, offs, out):
+    nc = tc.nc
+    with ExitStack() as ctx:
+        keep = ctx.enter_context(tc.tile_pool(name="keep", bufs=1))
+        psum = ctx.enter_context(tc.psum_pool(name="psum", bufs=1))
+
+        offsets = keep.tile([P, I // 16], U16, name="offsets")
+        nc.sync.dma_start(offsets[:], offs)
+
+        def load_rows(rows, name):
+            raw = keep.tile([P, PACK, Q], F32, name=name, tag=name)
+            nc.sync.dma_start(out=raw[:], in_=rows.rearrange("(p j) w -> p j w", j=PACK))
+            return raw
+
+        def load_words(words, name):
+            pool_words = keep.tile([P, T], U16, name=name)
+            nc.sync.dma_start(out=pool_words[:].bitcast(I32), in_=words[0].bitcast(I32))
+            return pool_words
+
+        def load_scales(engines, pool_scales, scales):
+            for r in range(4):
+                engines[r].dma_start(out=pool_scales[r:P:32, :].bitcast(I32), in_=scales[0, r:16:4, :].bitcast(I32))
+
+        def interleave(raw, name):
+            grouped = keep.tile([P, Q, PACK], BF16, name=name, align_bytes=64)
+            nc.scalar.activation(grouped[:], raw[:].rearrange("p j w -> p w j"), ACT.Copy)
+            return grouped
+
+        def quantize(grouped, name):
+            codes = keep.tile([P, Q], U32, name=name + "_codes", align_bytes=64)
+            scales = keep.tile([P, Q], U8, name=name + "_scales", align_bytes=64)
+            nc.vector.quantize_mx(out=codes[:].bitcast(FP8X4), scales=scales[:], in_=grouped[:].rearrange("p w j -> p (w j)"))
+            return codes, scales
+
+        def gather(window, dtype, name):
+            picked = keep.tile([P, I], dtype, name=name, align_bytes=64)
+            nc.vector.tensor_copy(picked[:], window[:].indirect(offsets[:]))
+            return picked
+
+        def product(rows, words, scales, name, width):
+            acc = psum.tile([Q, width], F32, name=name)
+            nc.tensor.matmul_mx(out=acc[:], lhsT=rows[0][:].bitcast(FP8X4), lhsT_scale=rows[1][:],
+                                rhs=words.bitcast(FP4X4), rhs_scale=scales, start=True, stop=True)
+            return acc
+
+        def column(name):
+            return keep.tile([P, 1], F32, name=name)
+
+        def slots(name):
+            return keep.tile([P, I], F32, name=name)
+
+        key_scale_pool = keep.tile([P, T], U8, name="key_scale_pool")
+        val_scale_pool = keep.tile([P, T], U8, name="val_scale_pool", tag="val_scale_pool")
+        placed = keep.tile([P, T], F32, name="placed")
+        nc.vector.memset(key_scale_pool[:].bitcast(I32), 0)
+        nc.vector.memset(val_scale_pool[:].bitcast(I32), 0)
+        nc.vector.memset(placed[:, : T // 2], 0.0)
+
+        query_raw = load_rows(query, "query_raw")
+        load_scales((nc.scalar, nc.scalar, nc.sync, nc.sync), key_scale_pool, keys_scales)
+        key_word_pool = load_words(keys_words, "key_word_pool")
+        gout_raw = load_rows(gout, "gout_raw")
+        load_scales((nc.sync,) * 4, val_scale_pool, vals_scales)
+        val_word_pool = load_words(vals_words, "val_word_pool")
+        old_sb = keep.tile([P, T], F32, name="old_sb")
+        nc.sync.dma_start(out=old_sb[:], in_=old)
+
+        s = column("s")
+        nc.gpsimd.dma_start(out=s[:], in_=share)
+        nc.gpsimd.memset(placed[:, T // 2 :], 0.0)
+        minus_one = column("minus_one")
+        nc.gpsimd.memset(minus_one[:], -1.0)
+        part_scale, part_bias, slope_scale, slope_bias = column("part_scale"), column("part_bias"), column("slope_scale"), column("slope_bias")
+        nc.gpsimd.tensor_scalar(part_scale[:], s[:], 1.5, -1.5, ALU.mult, ALU.add)
+        nc.gpsimd.tensor_scalar(part_bias[:], s[:], -0.5, 1.5, ALU.mult, ALU.add)
+        nc.gpsimd.tensor_scalar(slope_scale[:], s[:], -384.0, 384.0, ALU.mult, ALU.add)
+        nc.gpsimd.tensor_scalar(slope_bias[:], s[:], 512.0, 0.0, ALU.mult, ALU.add)
+
+        query_grouped = interleave(query_raw, "query_grouped")
+        gout_grouped = interleave(gout_raw, "gout_grouped")
+        key_scales = gather(key_scale_pool, U8, "key_scales")
+        query_mx = quantize(query_grouped, "query")
+        key_words = keep.tile([P, I], U16, name="key_words", align_bytes=64)
+        a_halves = []
+        for h in range(2):
+            cols = slice(h * HALF, (h + 1) * HALF)
+            nc.vector.tensor_copy(key_words[:, cols], key_word_pool[:].indirect(offsets[:, h * HALF // 16 : (h + 1) * HALF // 16]))
+            a_halves.append(product(query_mx, key_words[:, cols], key_scales[:, cols], "a%d" % h, HALF))
+        gout_mx = quantize(gout_grouped, "gout")
+        val_scales = gather(val_scale_pool, U8, "val_scales")
+
+        e, part, u2, slope = slots("e"), slots("part"), slots("u2"), slots("slope")
+        t = keep.tile([P, I], F32, name="t", tag="gout_raw")
+        neg_a = keep.tile([P, I], F32, name="neg_a", tag="val_scale_pool")
+        neg_max_first, neg_max = column("neg_max_first"), column("neg_max")
+        for h in range(2):
+            nc.scalar.activation(t[:, h * HALF : (h + 1) * HALF], a_halves[h][:], ACT.Tanh, scale=0.5)
+        nc.vector.tensor_scalar(neg_a[:, :HALF], a_halves[0][:], -1.0, None, ALU.mult, ALU.min, accum_out=neg_max_first[:])
+        nc.vector.tensor_scalar(neg_a[:, HALF:], a_halves[1][:], -1.0, neg_max_first[:], ALU.mult, ALU.min, accum_out=neg_max[:])
+        nc.scalar.activation(e[:], neg_a[:], ACT.Exp, bias=neg_max[:], scale=-1.0)
+        nc.scalar.activation(part[:], t[:], ACT.Identity, bias=part_bias[:], scale=part_scale[:])
+        nc.scalar.activation(u2[:], t[:], ACT.Square, bias=minus_one[:])
+        nc.scalar.activation(slope[:], u2[:], ACT.Identity, bias=slope_bias[:], scale=slope_scale[:])
+
+        val_words = gather(val_word_pool, U16, "val_words")
+        c0 = product(gout_mx, val_words[:], val_scales[:], "c0", I)
+
+        p, weighted, centred = slots("p"), slots("weighted"), slots("centred")
+        z, inv_z, mean = column("z"), column("inv_z"), column("mean")
+        nc.vector.scalar_tensor_tensor(p[:], part[:], 1.0, e[:], ALU.mult, ALU.mult, accum_out=z[:])
+        nc.vector.reciprocal(inv_z[:], z[:])
+        nc.vector.scalar_tensor_tensor(weighted[:], c0[:], inv_z[:], p[:], ALU.mult, ALU.mult, accum_out=mean[:])
+        nc.vector.scalar_tensor_tensor(centred[:], c0[:], mean[:], slope[:], ALU.subtract, ALU.mult)
+        nc.vector.tensor_tensor(placed[:].indirect(offsets[:]), centred[:], e[:], ALU.mult)
+
+        first = 0
+        for n, width in enumerate(STORE_WIDTHS):
+            cols = slice(first, first + width)
+            result = keep.tile([P, width], F32, name="result%d" % n)
+            nc.vector.scalar_tensor_tensor(result[:], placed[:, cols], inv_z[:], old_sb[:, cols], ALU.mult, ALU.add)
+            nc.sync.dma_start(out=out[:, cols], in_=result[:])
+            first = first + width

@@ -19,7 +19,7 @@ ACT = mybir.ActivationFunctionType
 P = 128
 PACK = 4
 HALF = I // 2
-STORE_WIDTHS = (256, 512, 512, 512, 256)
+STORE_WIDTHS = (256, 384, 384, 384, 384, 256)
 
 
 def tile_attend_bmixedparts_s_kernel(tc, query, keys_words, keys_scales, share, gout, vals_words, vals_scales, old, offs, out):
@@ -37,7 +37,7 @@ def tile_attend_bmixedparts_s_kernel(tc, query, keys_words, keys_scales, share, 
             return raw
 
         def load_words(words, name):
-            pool_words = keep.tile([P, T], U16, name=name)
+            pool_words = keep.tile([P, T], U16, name=name, tag=name, align_bytes=64)
             nc.sync.dma_start(out=pool_words[:].bitcast(I32), in_=words[0].bitcast(I32))
             return pool_words
 
@@ -50,8 +50,8 @@ def tile_attend_bmixedparts_s_kernel(tc, query, keys_words, keys_scales, share, 
             nc.scalar.activation(grouped[:], raw[:].rearrange("p j w -> p w j"), ACT.Copy)
             return grouped
 
-        def quantize(grouped, name):
-            codes = keep.tile([P, Q], U32, name=name + "_codes", align_bytes=64)
+        def quantize(grouped, name, tag):
+            codes = keep.tile([P, Q], U32, name=name + "_codes", tag=tag, align_bytes=64)
             scales = keep.tile([P, Q], U8, name=name + "_scales", align_bytes=64)
             nc.vector.quantize_mx(out=codes[:].bitcast(FP8X4), scales=scales[:], in_=grouped[:].rearrange("p w j -> p (w j)"))
             return codes, scales
@@ -78,58 +78,57 @@ def tile_attend_bmixedparts_s_kernel(tc, query, keys_words, keys_scales, share, 
         placed = keep.tile([P, T], F32, name="placed")
         nc.vector.memset(key_scale_pool[:].bitcast(I32), 0)
         nc.vector.memset(val_scale_pool[:].bitcast(I32), 0)
-        nc.vector.memset(placed[:, : T // 2], 0.0)
+        minus_one = column("minus_one")
+        nc.vector.memset(minus_one[:], -1.0)
+        nc.vector.memset(placed[:], 0.0)
 
         query_raw = load_rows(query, "query_raw")
         load_scales((nc.scalar, nc.scalar, nc.sync, nc.sync), key_scale_pool, keys_scales)
         key_word_pool = load_words(keys_words, "key_word_pool")
         gout_raw = load_rows(gout, "gout_raw")
-        load_scales((nc.sync,) * 4, val_scale_pool, vals_scales)
         val_word_pool = load_words(vals_words, "val_word_pool")
+        s = column("s")
+        nc.sync.dma_start(out=s[:], in_=share)
+        load_scales((nc.sync,) * 4, val_scale_pool, vals_scales)
         old_sb = keep.tile([P, T], F32, name="old_sb")
         nc.sync.dma_start(out=old_sb[:], in_=old)
-
-        s = column("s")
-        nc.gpsimd.dma_start(out=s[:], in_=share)
-        nc.gpsimd.memset(placed[:, T // 2 :], 0.0)
-        minus_one = column("minus_one")
-        nc.gpsimd.memset(minus_one[:], -1.0)
-        part_scale, part_bias, slope_scale, slope_bias = column("part_scale"), column("part_bias"), column("slope_scale"), column("slope_bias")
-        nc.gpsimd.tensor_scalar(part_scale[:], s[:], 1.5, -1.5, ALU.mult, ALU.add)
-        nc.gpsimd.tensor_scalar(part_bias[:], s[:], -0.5, 1.5, ALU.mult, ALU.add)
-        nc.gpsimd.tensor_scalar(slope_scale[:], s[:], -384.0, 384.0, ALU.mult, ALU.add)
-        nc.gpsimd.tensor_scalar(slope_bias[:], s[:], 512.0, 0.0, ALU.mult, ALU.add)
 
         query_grouped = interleave(query_raw, "query_grouped")
         gout_grouped = interleave(gout_raw, "gout_grouped")
         key_scales = gather(key_scale_pool, U8, "key_scales")
-        query_mx = quantize(query_grouped, "query")
+        query_mx = quantize(query_grouped, "query", "query_codes")
         key_words = keep.tile([P, I], U16, name="key_words", align_bytes=64)
         a_halves = []
         for h in range(2):
             cols = slice(h * HALF, (h + 1) * HALF)
             nc.vector.tensor_copy(key_words[:, cols], key_word_pool[:].indirect(offsets[:, h * HALF // 16 : (h + 1) * HALF // 16]))
             a_halves.append(product(query_mx, key_words[:, cols], key_scales[:, cols], "a%d" % h, HALF))
-        gout_mx = quantize(gout_grouped, "gout")
-        val_scales = gather(val_scale_pool, U8, "val_scales")
+        val_words = gather(val_word_pool, U16, "val_words")
 
         e, part, u2, slope = slots("e"), slots("part"), slots("u2"), slots("slope")
         t = keep.tile([P, I], F32, name="t", tag="gout_raw")
-        neg_a = keep.tile([P, I], F32, name="neg_a", tag="val_scale_pool")
+        neg_a = keep.tile([P, I], F32, name="neg_a")
         neg_max_first, neg_max = column("neg_max_first"), column("neg_max")
         for h in range(2):
             nc.scalar.activation(t[:, h * HALF : (h + 1) * HALF], a_halves[h][:], ACT.Tanh, scale=0.5)
         nc.vector.tensor_scalar(neg_a[:, :HALF], a_halves[0][:], -1.0, None, ALU.mult, ALU.min, accum_out=neg_max_first[:])
+        gout_mx = quantize(gout_grouped, "gout", "val_word_pool")
         nc.vector.tensor_scalar(neg_a[:, HALF:], a_halves[1][:], -1.0, neg_max_first[:], ALU.mult, ALU.min, accum_out=neg_max[:])
-        nc.scalar.activation(e[:], neg_a[:], ACT.Exp, bias=neg_max[:], scale=-1.0)
+        part_scale, part_bias, slope_scale, slope_bias = column("part_scale"), column("part_bias"), column("slope_scale"), column("slope_bias")
+        nc.scalar.activation(part_scale[:], s[:], ACT.Copy, bias=-1.5, scale=1.5)
+        nc.scalar.activation(part_bias[:], s[:], ACT.Copy, bias=1.5, scale=-0.5)
         nc.scalar.activation(part[:], t[:], ACT.Identity, bias=part_bias[:], scale=part_scale[:])
+        nc.scalar.activation(e[:], neg_a[:], ACT.Exp, bias=neg_max[:], scale=-1.0)
+        nc.scalar.activation(slope_scale[:], s[:], ACT.Copy, bias=384.0, scale=-384.0)
+        nc.scalar.activation(slope_bias[:], s[:], ACT.Copy, scale=512.0)
         nc.scalar.activation(u2[:], t[:], ACT.Square, bias=minus_one[:])
         nc.scalar.activation(slope[:], u2[:], ACT.Identity, bias=slope_bias[:], scale=slope_scale[:])
 
-        val_words = gather(val_word_pool, U16, "val_words")
+        val_scales = gather(val_scale_pool, U8, "val_scales")
         c0 = product(gout_mx, val_words[:], val_scales[:], "c0", I)
 
-        p, weighted, centred = slots("p"), slots("weighted"), slots("centred")
+        p = keep.tile([P, I], F32, name="p", tag="val_scale_pool")
+        weighted, centred = slots("weighted"), slots("centred")
         z, inv_z, mean = column("z"), column("inv_z"), column("mean")
         nc.vector.scalar_tensor_tensor(p[:], part[:], 1.0, e[:], ALU.mult, ALU.mult, accum_out=z[:])
         nc.vector.reciprocal(inv_z[:], z[:])

@@ -19,7 +19,7 @@ ACT = mybir.ActivationFunctionType
 P = 128
 PACK = 4
 HALF = I // 2
-STORE_WIDTHS = (256, 384, 384, 384, 384, 256)
+STORE_WIDTHS = (160, 256, 288, 320, 320, 320, 256, 128)
 
 
 def tile_attend_bmixedparts_s_kernel(tc, query, keys_words, keys_scales, share, gout, vals_words, vals_scales, old, offs, out):
@@ -47,7 +47,7 @@ def tile_attend_bmixedparts_s_kernel(tc, query, keys_words, keys_scales, share, 
 
         def interleave(raw, name):
             grouped = keep.tile([P, Q, PACK], BF16, name=name, align_bytes=64)
-            nc.scalar.activation(grouped[:], raw[:].rearrange("p j w -> p w j"), ACT.Copy)
+            nc.scalar.activation(grouped[:].rearrange("p (c i) j -> p c j i", i=4), raw[:].rearrange("p j (c i) -> p c j i", i=4), ACT.Copy)
             return grouped
 
         def quantize(grouped, name, tag):
@@ -128,18 +128,19 @@ def tile_attend_bmixedparts_s_kernel(tc, query, keys_words, keys_scales, share, 
         c0 = product(gout_mx, val_words[:], val_scales[:], "c0", I)
 
         p = keep.tile([P, I], F32, name="p", tag="val_scale_pool")
-        weighted, centred = slots("weighted"), slots("centred")
-        z, inv_z, mean = column("z"), column("inv_z"), column("mean")
+        weighted, w, centred = slots("weighted"), slots("w"), slots("centred")
+        z, inv_z, total = column("z"), column("inv_z"), column("total")
         nc.vector.scalar_tensor_tensor(p[:], part[:], 1.0, e[:], ALU.mult, ALU.mult, accum_out=z[:])
         nc.vector.reciprocal(inv_z[:], z[:])
-        nc.vector.scalar_tensor_tensor(weighted[:], c0[:], inv_z[:], p[:], ALU.mult, ALU.mult, accum_out=mean[:])
-        nc.vector.scalar_tensor_tensor(centred[:], c0[:], mean[:], slope[:], ALU.subtract, ALU.mult)
-        nc.vector.tensor_tensor(placed[:].indirect(offsets[:]), centred[:], e[:], ALU.mult)
+        nc.vector.scalar_tensor_tensor(weighted[:], c0[:], -1.0, p[:], ALU.mult, ALU.mult, accum_out=total[:])
+        nc.vector.scalar_tensor_tensor(w[:], slope[:], inv_z[:], e[:], ALU.mult, ALU.mult)
+        nc.scalar.activation(centred[:], c0[:], ACT.Identity, bias=total[:], scale=z[:])
+        nc.vector.tensor_tensor(placed[:].indirect(offsets[:]), centred[:], w[:], ALU.mult)
 
         first = 0
         for n, width in enumerate(STORE_WIDTHS):
             cols = slice(first, first + width)
             result = keep.tile([P, width], F32, name="result%d" % n)
             nc.vector.scalar_tensor_tensor(result[:], placed[:, cols], inv_z[:], old_sb[:, cols], ALU.mult, ALU.add)
-            nc.sync.dma_start(out=out[:, cols], in_=result[:])
+            (nc.sync, nc.scalar)[n % 2].dma_start(out=out[:, cols], in_=result[:])
             first = first + width

from contextlib import ExitStack

import concourse.mybir as mybir

D, E, T, I, Q = 512, 512, 2048, 512, 128
FLOPS = 2 * Q * I * (D + E)

F32 = mybir.dt.float32
BF16 = mybir.dt.bfloat16
I32 = mybir.dt.int32
U32 = mybir.dt.uint32
U16 = mybir.dt.uint16
U8 = mybir.dt.uint8
FP8X4 = mybir.dt.float8_e4m3fn_x4
FP4X4 = mybir.dt.float4_e2m1fn_x4
ALU = mybir.AluOpType
ACT = mybir.ActivationFunctionType

P = 128
PACK = 4
HALF = I // 2
STORE_WIDTHS = (160, 256, 288, 320, 320, 320, 256, 128)


def tile_attend_bmixedparts_s_kernel(tc, query, keys_words, keys_scales, share, gout, vals_words, vals_scales, old, offs, out):
    nc = tc.nc
    with ExitStack() as ctx:
        keep = ctx.enter_context(tc.tile_pool(name="keep", bufs=1))
        psum = ctx.enter_context(tc.psum_pool(name="psum", bufs=1))

        offsets = keep.tile([P, I // 16], U16, name="offsets")
        nc.sync.dma_start(offsets[:], offs)

        def load_rows(rows, name):
            raw = keep.tile([P, PACK, Q], F32, name=name, tag=name)
            nc.sync.dma_start(out=raw[:], in_=rows.rearrange("(p j) w -> p j w", j=PACK))
            return raw

        def load_words(words, name):
            pool_words = keep.tile([P, T], U16, name=name, tag=name, align_bytes=64)
            nc.sync.dma_start(out=pool_words[:].bitcast(I32), in_=words[0].bitcast(I32))
            return pool_words

        def load_scales(engines, pool_scales, scales):
            for r in range(4):
                engines[r].dma_start(out=pool_scales[r:P:32, :].bitcast(I32), in_=scales[0, r:16:4, :].bitcast(I32))

        def interleave(raw, name):
            grouped = keep.tile([P, Q, PACK], BF16, name=name, align_bytes=64)
            nc.scalar.activation(grouped[:].rearrange("p (c i) j -> p c j i", i=4), raw[:].rearrange("p j (c i) -> p c j i", i=4), ACT.Copy)
            return grouped

        def quantize(grouped, name, tag):
            codes = keep.tile([P, Q], U32, name=name + "_codes", tag=tag, align_bytes=64)
            scales = keep.tile([P, Q], U8, name=name + "_scales", align_bytes=64)
            nc.vector.quantize_mx(out=codes[:].bitcast(FP8X4), scales=scales[:], in_=grouped[:].rearrange("p w j -> p (w j)"))
            return codes, scales

        def gather(window, dtype, name):
            picked = keep.tile([P, I], dtype, name=name, align_bytes=64)
            nc.vector.tensor_copy(picked[:], window[:].indirect(offsets[:]))
            return picked

        def product(rows, words, scales, name, width):
            acc = psum.tile([Q, width], F32, name=name)
            nc.tensor.matmul_mx(out=acc[:], lhsT=rows[0][:].bitcast(FP8X4), lhsT_scale=rows[1][:],
                                rhs=words.bitcast(FP4X4), rhs_scale=scales, start=True, stop=True)
            return acc

        def column(name):
            return keep.tile([P, 1], F32, name=name)

        def slots(name):
            return keep.tile([P, I], F32, name=name)

        key_scale_pool = keep.tile([P, T], U8, name="key_scale_pool")
        val_scale_pool = keep.tile([P, T], U8, name="val_scale_pool", tag="val_scale_pool")
        placed = keep.tile([P, T], F32, name="placed")
        nc.vector.memset(key_scale_pool[:].bitcast(I32), 0)
        nc.vector.memset(val_scale_pool[:].bitcast(I32), 0)
        minus_one = column("minus_one")
        nc.vector.memset(minus_one[:], -1.0)
        nc.vector.memset(placed[:], 0.0)

        query_raw = load_rows(query, "query_raw")
        load_scales((nc.scalar, nc.scalar, nc.sync, nc.sync), key_scale_pool, keys_scales)
        key_word_pool = load_words(keys_words, "key_word_pool")
        gout_raw = load_rows(gout, "gout_raw")
        val_word_pool = load_words(vals_words, "val_word_pool")
        s = column("s")
        nc.sync.dma_start(out=s[:], in_=share)
        load_scales((nc.sync,) * 4, val_scale_pool, vals_scales)
        old_sb = keep.tile([P, T], F32, name="old_sb")
        nc.sync.dma_start(out=old_sb[:], in_=old)

        query_grouped = interleave(query_raw, "query_grouped")
        gout_grouped = interleave(gout_raw, "gout_grouped")
        key_scales = gather(key_scale_pool, U8, "key_scales")
        query_mx = quantize(query_grouped, "query", "query_codes")
        key_words = keep.tile([P, I], U16, name="key_words", align_bytes=64)
        a_halves = []
        for h in range(2):
            cols = slice(h * HALF, (h + 1) * HALF)
            nc.vector.tensor_copy(key_words[:, cols], key_word_pool[:].indirect(offsets[:, h * HALF // 16 : (h + 1) * HALF // 16]))
            a_halves.append(product(query_mx, key_words[:, cols], key_scales[:, cols], "a%d" % h, HALF))
        val_words = gather(val_word_pool, U16, "val_words")

        e, part, u2, slope = slots("e"), slots("part"), slots("u2"), slots("slope")
        t = keep.tile([P, I], F32, name="t", tag="gout_raw")
        neg_a = keep.tile([P, I], F32, name="neg_a")
        neg_max_first, neg_max = column("neg_max_first"), column("neg_max")
        for h in range(2):
            nc.scalar.activation(t[:, h * HALF : (h + 1) * HALF], a_halves[h][:], ACT.Tanh, scale=0.5)
        nc.vector.tensor_scalar(neg_a[:, :HALF], a_halves[0][:], -1.0, None, ALU.mult, ALU.min, accum_out=neg_max_first[:])
        gout_mx = quantize(gout_grouped, "gout", "val_word_pool")
        nc.vector.tensor_scalar(neg_a[:, HALF:], a_halves[1][:], -1.0, neg_max_first[:], ALU.mult, ALU.min, accum_out=neg_max[:])
        part_scale, part_bias, slope_scale, slope_bias = column("part_scale"), column("part_bias"), column("slope_scale"), column("slope_bias")
        nc.scalar.activation(part_scale[:], s[:], ACT.Copy, bias=-1.5, scale=1.5)
        nc.scalar.activation(part_bias[:], s[:], ACT.Copy, bias=1.5, scale=-0.5)
        nc.scalar.activation(part[:], t[:], ACT.Identity, bias=part_bias[:], scale=part_scale[:])
        nc.scalar.activation(e[:], neg_a[:], ACT.Exp, bias=neg_max[:], scale=-1.0)
        nc.scalar.activation(slope_scale[:], s[:], ACT.Copy, bias=384.0, scale=-384.0)
        nc.scalar.activation(slope_bias[:], s[:], ACT.Copy, scale=512.0)
        nc.scalar.activation(u2[:], t[:], ACT.Square, bias=minus_one[:])
        nc.scalar.activation(slope[:], u2[:], ACT.Identity, bias=slope_bias[:], scale=slope_scale[:])

        val_scales = gather(val_scale_pool, U8, "val_scales")
        c0 = product(gout_mx, val_words[:], val_scales[:], "c0", I)

        p = keep.tile([P, I], F32, name="p", tag="val_scale_pool")
        weighted, w, centred = slots("weighted"), slots("w"), slots("centred")
        z, inv_z, total = column("z"), column("inv_z"), column("total")
        nc.vector.scalar_tensor_tensor(p[:], part[:], 1.0, e[:], ALU.mult, ALU.mult, accum_out=z[:])
        nc.vector.reciprocal(inv_z[:], z[:])
        nc.vector.scalar_tensor_tensor(weighted[:], c0[:], -1.0, p[:], ALU.mult, ALU.mult, accum_out=total[:])
        nc.vector.scalar_tensor_tensor(w[:], slope[:], inv_z[:], e[:], ALU.mult, ALU.mult)
        nc.scalar.activation(centred[:], c0[:], ACT.Identity, bias=total[:], scale=z[:])
        nc.vector.tensor_tensor(placed[:].indirect(offsets[:]), centred[:], w[:], ALU.mult)

        first = 0
        for n, width in enumerate(STORE_WIDTHS):
            cols = slice(first, first + width)
            result = keep.tile([P, width], F32, name="result%d" % n)
            nc.vector.scalar_tensor_tensor(result[:], placed[:, cols], inv_z[:], old_sb[:, cols], ALU.mult, ALU.add)
            (nc.sync, nc.scalar)[n % 2].dma_start(out=out[:, cols], in_=result[:])
            first = first + width
